import numpy as np
import ml_dtypes


def mxq(x, axis, fmt="e4m3"):
    dtype, down = {"e4m3": (ml_dtypes.float8_e4m3fn, 7), "e5m2": (ml_dtypes.float8_e5m2, 14)}[fmt]
    v = np.moveaxis(np.asarray(x, np.float32).astype(ml_dtypes.bfloat16).astype(np.float64), axis, -1)
    blocks = v.reshape(v.shape[:-1] + (-1, 32))
    amax = np.abs(blocks).max(-1, keepdims=True)
    byte = np.maximum(np.where(amax > 0, np.frexp(amax)[1] - 1 + 127, 0) - down, 1)
    scale = np.exp2(byte - 127.0)
    codes = (blocks / scale).astype(np.float32).astype(dtype).astype(np.float64)
    return np.moveaxis((codes * scale).reshape(v.shape), -1, axis)


WIDE = False


def mx_kscale(k):
    if not WIDE:
        return np.ones(k)
    levels = np.array([30, -30])
    if k % 512:
        return np.exp2(np.random.permutation(np.resize(levels, k // 32))).repeat(32)
    a = np.empty((k // 512, 16))
    for p in range(k // 512):
        a[p, :8] = np.random.permutation(np.resize(levels, 8))
        for g in range(8):
            far = levels[np.abs(levels - a[p, g]) >= 10]
            a[p, g + 8] = far[np.random.randint(len(far))]
    return np.exp2(a.ravel()).repeat(32)


def f64(x):
    return np.asarray(x).astype(np.float64)


def striped(idx):
    return np.tile(np.asarray(idx).reshape(-1, 16).T, (8, 1)).astype(np.uint16)


def unstriped(offs):
    return offs[:16].T.reshape(-1).astype(np.int64)


E2M1 = np.array([0.0, 0.5, 1.0, 1.5, 2.0, 3.0, 4.0, 6.0, -0.0, -0.5, -1.0, -1.5, -2.0, -3.0, -4.0, -6.0])


def pack_weight(w, fmt):
    k, n = w.shape
    w = f64(np.asarray(w, np.float32).astype(ml_dtypes.bfloat16)).reshape(k // 32, 32, n)
    amax = np.abs(w).max(1)
    if fmt in ("e4m3", "e5m2"):
        byte = np.frexp(amax)[1] - 1 + 127 - (7 if fmt == "e4m3" else 14)
    else:
        mant, ex = np.frexp(amax / 6.0)
        byte = np.where(mant > 0.5, ex, ex - 1) + 127
    byte = np.clip(np.where(amax > 0, byte, 1), 1, 254)
    scaled = (w * np.exp2(127.0 - byte)[:, None, :]).reshape(k, n).astype(np.float32)
    by_word = np.ascontiguousarray(scaled.reshape(k // 512, 128, 4, n).transpose(0, 1, 3, 2))
    if fmt in ("e4m3", "e5m2"):
        words = by_word.astype(ml_dtypes.float8_e4m3fn if fmt == "e4m3" else ml_dtypes.float8_e5m2).view(np.uint8)
    else:
        c = by_word.astype(ml_dtypes.float4_e2m1fn).view(np.uint8) & 0xF
        words = (c[..., 0::2] | (c[..., 1::2] << 4)).reshape(k // 512, 128, 2 * n)
    return np.ascontiguousarray(words), np.ascontiguousarray(byte.astype(np.uint8).reshape(k // 512, 16, n))


def unpack_weight(words, scales, fmt):
    g, _, n = scales.shape
    words = np.ascontiguousarray(words).reshape(g, 128, n, -1)
    if fmt in ("e4m3", "e5m2"):
        vals = words.view(ml_dtypes.float8_e4m3fn if fmt == "e4m3" else ml_dtypes.float8_e5m2).astype(np.float64)
    else:
        nib = np.empty((g, 128, n, 4), np.uint8)
        nib[..., 0::2] = words & 0xF
        nib[..., 1::2] = words >> 4
        vals = E2M1[nib]
    vals = vals * np.repeat(np.exp2(scales.astype(np.float64) - 127.0), 8, axis=1)[..., None]
    return vals.transpose(0, 1, 3, 2).reshape(g * 512, n)


K, T, J, R, N, Z = 512, 1024, 256, 512, 256, 512


def setup_inputs():
    n = np.random.standard_normal
    idx = np.random.permutation(T)[:J]
    idx2 = np.random.permutation(Z)[:J]
    fk = mx_kscale(K)
    fr = mx_kscale(R)
    wp = pack_weight(n((K, R)) * 1 / np.sqrt(K) * fk[:, None] * fr, "e5m2")
    return {
        "xf": (n((K, T))).astype(np.float32),
        "fk": (np.random.uniform(0.5, 2.0, (K, 1)) / fk[:, None]).astype(np.float32),
        "w_words": wp[0],
        "w_scales": wp[1],
        "wb": (n((R, N)) * 1 / np.sqrt(R) / fr[:, None]).astype(np.float32),
        "tz": (n((N, Z)) * 0.6).astype(np.float32),
        "rw": (np.random.uniform(0.5, 2.0, (1, J))).astype(np.float32),
        "offs": striped(idx),
        "offs2": striped(idx2),
    }


def reference(xf, fk, w_words, w_scales, wb, tz, rw, offs, offs2):
    idx = unstriped(offs)
    idx2 = unstriped(offs2)
    wu = unpack_weight(w_words, w_scales, "e5m2")
    xg = f64(xf)[:, idx]
    x1 = np.pad(xg, ((0, 0), (1, 0)))[:, :J]
    u = (xg - 0.6 * x1) * f64(fk)
    uq = mxq(u, 0, "e4m3")
    a = wu.T @ uq
    ha = np.maximum(a, 0.0)
    h1 = np.pad(ha, ((0, 0), (2, 0)))[:, :J]
    hid = ha - 0.5 * h1
    wbq = mxq(f64(wb), 0, "e5m2")
    hidq = mxq(hid, 0, "e5m2")
    p = wbq.T @ hidq
    y = np.maximum(p, f64(tz)[:, idx2]) * f64(rw)
    return y

@@ -1,0 +1,217 @@
+from contextlib import ExitStack
+
+import concourse.mybir as mybir
+from concourse.masks import make_identity
+
+K, T, J, R, N, Z = 512, 1024, 256, 512, 256, 512
+FLOPS = 2 * K * R * J + 2 * R * N * J
+
+F32 = mybir.dt.float32
+BF16 = mybir.dt.bfloat16
+I32 = mybir.dt.int32
+U32 = mybir.dt.uint32
+U16 = mybir.dt.uint16
+U8 = mybir.dt.uint8
+E4M3X4 = mybir.dt.float8_e4m3fn_x4
+E5M2X4 = mybir.dt.float8_e5m2_x4
+ALU = mybir.AluOpType
+ACT = mybir.ActivationFunctionType
+
+P = 128
+PACK = 4
+HALF = 128
+HALVES = J // HALF
+N_TILES = N // P
+PAD = 8
+LAG = 2
+
+
+def tile_list_steps_lagged_floored_kernel(tc, xf, fk, w_words, w_scales, wb, tz, rw, offs, offs2, out):
+    nc = tc.nc
+    with ExitStack() as ctx:
+        sb = ctx.enter_context(tc.tile_pool(name="sb", bufs=1))
+        ps = ctx.enter_context(tc.psum_pool(name="ps", bufs=1))
+
+        x_list = sb.tile([P, J // 16], U16, name="x_list")
+        z_list = sb.tile([P, J // 16], U16, name="z_list")
+        x_plane = [sb.tile([P, T], F32, name="x_plane%d" % t) for t in range(PACK)]
+        fk_sb = sb.tile([P, PACK], F32, name="fk_sb")
+        rw_sb = sb.tile([P, 2], F32, name="rw_sb")
+        w_raw = sb.tile([P, R], I32, name="w_raw")
+        ws_raw = sb.tile([P, R], U8, name="ws_raw")
+        wb_raw = sb.tile([P, PACK, N], F32, name="wb_raw")
+        tz_sb = sb.tile([P, N_TILES, Z], F32, name="tz_sb")
+        picked = [sb.tile([P, PAD + J], F32, name="picked%d" % t) for t in range(PACK)]
+        half_relu = sb.tile([P, (LAG + J) * PACK], F32, name="half_relu")
+        ident = sb.tile([P, P], F32, name="ident")
+
+        x_rows = xf.rearrange("(p t) c -> t p c", t=PACK)
+
+        nc.gpsimd.memset(ws_raw[:].bitcast(U32), 0)
+        for t in range(PACK):
+            nc.vector.memset(picked[t][:, PAD - 1 : PAD], 0.0)
+        nc.vector.memset(half_relu[:, 0 : LAG * PACK], 0.0)
+
+        nc.sync.dma_start(out=w_raw[:], in_=w_words[0].rearrange("p n t -> p (n t)").bitcast(I32))
+        nc.scalar.dma_start(out=fk_sb[:], in_=fk.rearrange("(p t) o -> p (t o)", t=PACK))
+        nc.sync.dma_start(out=x_plane[0][:], in_=x_rows[0])
+        nc.sync.dma_start(x_list[:], offs)
+        for q in range(4):
+            nc.scalar.dma_start(
+                out=ws_raw[32 * q : 32 * q + 4, :].bitcast(I32),
+                in_=w_scales[0, 4 * q : 4 * q + 4, :].bitcast(I32),
+            )
+        for t in range(1, PACK):
+            nc.sync.dma_start(out=x_plane[t][:], in_=x_rows[t])
+        nc.sync.dma_start(out=wb_raw[:], in_=wb.rearrange("(p t) n -> p t n", t=PACK))
+        nc.sync.dma_start(z_list[:], offs2)
+        nc.sync.dma_start(out=tz_sb[:], in_=tz.rearrange("(c p) z -> p c z", p=P))
+        nc.gpsimd.dma_start(out=rw_sb[:], in_=rw.rearrange("o (p c) -> p (o c)", c=2))
+        make_identity(nc, ident[:])
+
+        step = [sb.tile([P, J], F32, name="step%d" % t) for t in range(PACK)]
+        u_bf = [sb.tile([P, HALF, PACK], BF16, name="u_bf%d" % h, tag="u_bf%d" % h, align_bytes=64) for h in range(HALVES)]
+        u_codes = [sb.tile([P, HALF], U32, name="u_codes%d" % h, tag="u_codes%d" % h, align_bytes=64) for h in range(HALVES)]
+        u_scales = [sb.tile([P, HALF], U8, name="u_scales%d" % h, align_bytes=64) for h in range(HALVES)]
+        w_codes = sb.tile([P, R], I32, name="w_codes", align_bytes=64)
+        w_planes = sb.tile([P, R], U8, name="w_planes", align_bytes=64)
+
+        def difference(t, j0, n):
+            nc.vector.scalar_tensor_tensor(
+                out=step[t][:, j0 : j0 + n],
+                in0=picked[t][:, PAD - 1 + j0 : PAD - 1 + j0 + n],
+                scalar=-0.6,
+                in1=picked[t][:, PAD + j0 : PAD + j0 + n],
+                op0=ALU.mult,
+                op1=ALU.add,
+            )
+
+        def scale_round(t, h):
+            nc.vector.tensor_scalar(
+                out=u_bf[h][:, :, t],
+                in0=step[t][:, h * HALF : (h + 1) * HALF],
+                scalar1=fk_sb[:, t : t + 1],
+                scalar2=None,
+                op0=ALU.mult,
+            )
+
+        nc.vector.tensor_copy(
+            out=w_codes[:].rearrange("p (t m) -> p m t", t=PACK),
+            in_=w_raw[:].rearrange("p (m t) -> p m t", t=PACK),
+        )
+        nc.vector.tensor_copy(
+            out=w_planes[:].rearrange("p (t m) -> p m t", t=PACK),
+            in_=ws_raw[:].rearrange("p (m t) -> p m t", t=PACK),
+        )
+        for t in range(PACK - 1):
+            nc.scalar.activation(picked[t][:, PAD:], x_plane[t][:].indirect(x_list[:]), ACT.Copy)
+            difference(t, 0, J)
+            for h in range(HALVES):
+                scale_round(t, h)
+        last = PACK - 1
+        cols = HALF // 16
+        for h in range(HALVES):
+            nc.scalar.activation(
+                picked[last][:, PAD + h * HALF : PAD + (h + 1) * HALF],
+                x_plane[last][:].indirect(x_list[:, h * cols : (h + 1) * cols]),
+                ACT.Copy,
+            )
+
+        def quantize(codes, scales, src, dtype):
+            nc.vector.quantize_mx(out=codes[:].bitcast(dtype), scales=scales[:], in_=src[:].rearrange("p c t -> p (c t)"))
+
+        for h in range(HALVES):
+            difference(last, h * HALF, HALF)
+            scale_round(last, h)
+            quantize(u_codes[h], u_scales[h], u_bf[h], E4M3X4)
+
+        rw_ps = ps.tile([P, 2, P], F32, name="rw_ps")
+        for c in range(2):
+            nc.tensor.transpose(rw_ps[:, c, :], rw_sb[:, c : c + 1].to_broadcast([P, P]), ident[:])
+
+        a_ps = [ps.tile([P, PACK, HALF], F32, name="a_ps%d" % h) for h in range(HALVES)]
+        for h in range(HALVES):
+            for t in range(PACK):
+                nc.tensor.matmul_mx(
+                    out=a_ps[h][:, t, :],
+                    lhsT=w_codes[:, t * P : (t + 1) * P].bitcast(E5M2X4),
+                    lhsT_scale=w_planes[:, t * P : (t + 1) * P],
+                    rhs=u_codes[h][:].bitcast(E4M3X4),
+                    rhs_scale=u_scales[h][:],
+                    start=True,
+                    stop=True,
+                )
+
+        wb_bf = [
+            sb.tile([P, P, PACK], BF16, name="wb_bf0", align_bytes=64),
+            sb.tile([P, P, PACK], BF16, name="wb_bf1", tag="u_bf1", align_bytes=64),
+        ]
+        wb_codes = [sb.tile([P, P], U32, name="wb_codes%d" % c, align_bytes=64) for c in range(N_TILES)]
+        wb_scales = [sb.tile([P, P], U8, name="wb_scales%d" % c, align_bytes=64) for c in range(N_TILES)]
+        for c, copy in enumerate((nc.scalar.copy, nc.vector.tensor_copy)):
+            copy(
+                wb_bf[c][:].rearrange("p (g i) t -> p g t i", i=4),
+                wb_raw[:, :, c * P : (c + 1) * P].rearrange("p t (g i) -> p g t i", i=4),
+            )
+        for c in range(N_TILES):
+            quantize(wb_codes[c], wb_scales[c], wb_bf[c], E5M2X4)
+
+        hid_bf = [sb.tile([P, HALF, PACK], BF16, name="hid_bf%d" % h, align_bytes=64) for h in range(HALVES)]
+        hid_codes = [sb.tile([P, HALF], U32, name="hid_codes%d" % h, align_bytes=64) for h in range(HALVES)]
+        hid_scales = [sb.tile([P, HALF], U8, name="hid_scales%d" % h, align_bytes=64) for h in range(HALVES)]
+        width = HALF * PACK
+        for h in range(HALVES):
+            lo = LAG * PACK + h * width
+            nc.scalar.activation(
+                half_relu[:, lo : lo + width].rearrange("p (j t) -> p j t", t=PACK),
+                a_ps[h][:].rearrange("p t j -> p j t"),
+                ACT.Relu,
+                scale=0.5,
+            )
+        for h in range(HALVES):
+            nc.vector.scalar_tensor_tensor(
+                out=hid_bf[h][:],
+                in0=a_ps[h][:].rearrange("p t j -> p j t"),
+                scalar=0.0,
+                in1=half_relu[:, h * width : (h + 1) * width].rearrange("p (j t) -> p j t", t=PACK),
+                op0=ALU.max,
+                op1=ALU.subtract,
+            )
+        floor_all = sb.tile([P, HALVES, N_TILES, HALF], F32, name="floor_all", tag="u_codes1", align_bytes=64)
+        floor_sb = [floor_all[:, h] for h in range(HALVES)]
+        for h in range(HALVES):
+            for c in range(N_TILES):
+                nc.scalar.activation(
+                    floor_sb[h][:, c, :], tz_sb[:, c, :].indirect(z_list[:, h * cols : (h + 1) * cols]), ACT.Copy
+                )
+        for h in range(HALVES):
+            quantize(hid_codes[h], hid_scales[h], hid_bf[h], E5M2X4)
+
+        p_ps = [ps.tile([P, N_TILES, HALF], F32, name="p_ps%d" % h) for h in range(HALVES)]
+        for h in range(HALVES):
+            for c in range(N_TILES):
+                nc.tensor.matmul_mx(
+                    out=p_ps[h][:, c, :],
+                    lhsT=wb_codes[c][:].bitcast(E5M2X4),
+                    lhsT_scale=wb_scales[c][:],
+                    rhs=hid_codes[h][:].bitcast(E5M2X4),
+                    rhs_scale=hid_scales[h][:],
+                    start=True,
+                    stop=True,
+                )
+
+        out_rows = out.rearrange("(c p) j -> p c j", p=P)
+        higher = [sb.tile([P, N_TILES, HALF], F32, name="higher%d" % h) for h in range(HALVES)]
+        result = [sb.tile([P, N_TILES, HALF], F32, name="result%d" % h) for h in range(HALVES)]
+        pairs = HALF // 2
+        for h in range(HALVES):
+            nc.vector.tensor_tensor(out=higher[h][:], in0=p_ps[h][:], in1=floor_sb[h], op=ALU.max)
+        for h in range(HALVES):
+            weights = rw_ps[:, :, h * pairs : (h + 1) * pairs].rearrange("p e m -> p m e")
+            nc.vector.tensor_tensor(
+                out=result[h][:].rearrange("p c (m e) -> p c m e", e=2),
+                in0=higher[h][:].rearrange("p c (m e) -> p c m e", e=2),
+                in1=weights.unsqueeze(1).to_broadcast([P, N_TILES, pairs, 2]),
+                op=ALU.mult,
+            )
+            nc.sync.dma_start(out=out_rows[:, :, h * HALF : (h + 1) * HALF], in_=result[h][:])

@@ -24,6 +24,7 @@ HALVES = J // HALF
 N_TILES = N // P
 PAD = 8
 LAG = 2
+CHUNK = 64
 
 
 def tile_list_steps_lagged_floored_kernel(tc, xf, fk, w_words, w_scales, wb, tz, rw, offs, offs2, out):
@@ -50,10 +51,12 @@ def tile_list_steps_lagged_floored_kernel(tc, xf, fk, w_words, w_scales, wb, tz,
         nc.gpsimd.memset(ws_raw[:].bitcast(U32), 0)
         for t in range(PACK):
             nc.vector.memset(picked[t][:, PAD - 1 : PAD], 0.0)
-        nc.vector.memset(half_relu[:, 0 : LAG * PACK], 0.0)
+        nc.scalar.activation(
+            half_relu[:, 0 : LAG * PACK], picked[0][:, PAD - 1 : PAD].to_broadcast([P, LAG * PACK]), ACT.Relu
+        )
 
-        nc.sync.dma_start(out=w_raw[:], in_=w_words[0].rearrange("p n t -> p (n t)").bitcast(I32))
         nc.scalar.dma_start(out=fk_sb[:], in_=fk.rearrange("(p t) o -> p (t o)", t=PACK))
+        nc.scalar.dma_start(out=rw_sb[:], in_=rw.rearrange("o (p c) -> p (o c)", c=2))
         nc.sync.dma_start(out=x_plane[0][:], in_=x_rows[0])
         nc.sync.dma_start(x_list[:], offs)
         for q in range(4):
@@ -63,10 +66,10 @@ def tile_list_steps_lagged_floored_kernel(tc, xf, fk, w_words, w_scales, wb, tz,
             )
         for t in range(1, PACK):
             nc.sync.dma_start(out=x_plane[t][:], in_=x_rows[t])
+        nc.sync.dma_start(out=w_raw[:], in_=w_words[0].rearrange("p n t -> p (n t)").bitcast(I32))
         nc.sync.dma_start(out=wb_raw[:], in_=wb.rearrange("(p t) n -> p t n", t=PACK))
         nc.sync.dma_start(z_list[:], offs2)
         nc.sync.dma_start(out=tz_sb[:], in_=tz.rearrange("(c p) z -> p c z", p=P))
-        nc.gpsimd.dma_start(out=rw_sb[:], in_=rw.rearrange("o (p c) -> p (o c)", c=2))
         make_identity(nc, ident[:])
 
         step = [sb.tile([P, J], F32, name="step%d" % t) for t in range(PACK)]
@@ -96,34 +99,35 @@ def tile_list_steps_lagged_floored_kernel(tc, xf, fk, w_words, w_scales, wb, tz,
             )
 
         nc.vector.tensor_copy(
-            out=w_codes[:].rearrange("p (t m) -> p m t", t=PACK),
-            in_=w_raw[:].rearrange("p (m t) -> p m t", t=PACK),
-        )
-        nc.vector.tensor_copy(
             out=w_planes[:].rearrange("p (t m) -> p m t", t=PACK),
             in_=ws_raw[:].rearrange("p (m t) -> p m t", t=PACK),
         )
-        for t in range(PACK - 1):
-            nc.scalar.activation(picked[t][:, PAD:], x_plane[t][:].indirect(x_list[:]), ACT.Copy)
-            difference(t, 0, J)
-            for h in range(HALVES):
-                scale_round(t, h)
-        last = PACK - 1
         cols = HALF // 16
-        for h in range(HALVES):
-            nc.scalar.activation(
-                picked[last][:, PAD + h * HALF : PAD + (h + 1) * HALF],
-                x_plane[last][:].indirect(x_list[:, h * cols : (h + 1) * cols]),
-                ACT.Copy,
-            )
+        last = PACK - 1
+        for t in range(PACK):
+            for h in range(HALVES):
+                nc.scalar.activation(
+                    picked[t][:, PAD + h * HALF : PAD + (h + 1) * HALF],
+                    x_plane[t][:].indirect(x_list[:, h * cols : (h + 1) * cols]),
+                    ACT.Copy,
+                )
+                if t < last:
+                    difference(t, h * HALF, HALF)
+                    scale_round(t, h)
 
         def quantize(codes, scales, src, dtype):
             nc.vector.quantize_mx(out=codes[:].bitcast(dtype), scales=scales[:], in_=src[:].rearrange("p c t -> p (c t)"))
 
-        for h in range(HALVES):
-            difference(last, h * HALF, HALF)
-            scale_round(last, h)
-            quantize(u_codes[h], u_scales[h], u_bf[h], E4M3X4)
+        difference(last, 0, HALF)
+        nc.vector.tensor_copy(
+            out=w_codes[:].rearrange("p (t m) -> p m t", t=PACK),
+            in_=w_raw[:].rearrange("p (m t) -> p m t", t=PACK),
+        )
+        scale_round(last, 0)
+        quantize(u_codes[0], u_scales[0], u_bf[0], E4M3X4)
+        difference(last, HALF, HALF)
+        scale_round(last, 1)
+        quantize(u_codes[1], u_scales[1], u_bf[1], E4M3X4)
 
         rw_ps = ps.tile([P, 2, P], F32, name="rw_ps")
         for c in range(2):
@@ -142,41 +146,37 @@ def tile_list_steps_lagged_floored_kernel(tc, xf, fk, w_words, w_scales, wb, tz,
                     stop=True,
                 )
 
-        wb_bf = [
-            sb.tile([P, P, PACK], BF16, name="wb_bf0", align_bytes=64),
-            sb.tile([P, P, PACK], BF16, name="wb_bf1", tag="u_bf1", align_bytes=64),
-        ]
+        wb_bf = [sb.tile([P, P, PACK], BF16, name="wb_bf%d" % c, align_bytes=64) for c in range(N_TILES)]
         wb_codes = [sb.tile([P, P], U32, name="wb_codes%d" % c, align_bytes=64) for c in range(N_TILES)]
         wb_scales = [sb.tile([P, P], U8, name="wb_scales%d" % c, align_bytes=64) for c in range(N_TILES)]
-        for c, copy in enumerate((nc.scalar.copy, nc.vector.tensor_copy)):
-            copy(
+        for c in range(N_TILES):
+            nc.scalar.copy(
                 wb_bf[c][:].rearrange("p (g i) t -> p g t i", i=4),
                 wb_raw[:, :, c * P : (c + 1) * P].rearrange("p t (g i) -> p g t i", i=4),
             )
-        for c in range(N_TILES):
             quantize(wb_codes[c], wb_scales[c], wb_bf[c], E5M2X4)
 
-        hid_bf = [sb.tile([P, HALF, PACK], BF16, name="hid_bf%d" % h, align_bytes=64) for h in range(HALVES)]
+        hid_bf = [sb.tile([P, HALF, PACK], BF16, name="hid_bf%d" % h, tag="hid_bf%d" % h, align_bytes=64) for h in range(HALVES)]
         hid_codes = [sb.tile([P, HALF], U32, name="hid_codes%d" % h, align_bytes=64) for h in range(HALVES)]
         hid_scales = [sb.tile([P, HALF], U8, name="hid_scales%d" % h, align_bytes=64) for h in range(HALVES)]
-        width = HALF * PACK
-        for h in range(HALVES):
-            lo = LAG * PACK + h * width
+        for j0 in range(0, J, CHUNK):
+            h, i0 = divmod(j0, HALF)
+            lo = (LAG + j0) * PACK
             nc.scalar.activation(
-                half_relu[:, lo : lo + width].rearrange("p (j t) -> p j t", t=PACK),
-                a_ps[h][:].rearrange("p t j -> p j t"),
+                half_relu[:, lo : lo + CHUNK * PACK].rearrange("p (j t) -> p j t", t=PACK),
+                a_ps[h][:, :, i0 : i0 + CHUNK].rearrange("p t j -> p j t"),
                 ACT.Relu,
-                scale=0.5,
             )
-        for h in range(HALVES):
             nc.vector.scalar_tensor_tensor(
-                out=hid_bf[h][:],
-                in0=a_ps[h][:].rearrange("p t j -> p j t"),
-                scalar=0.0,
-                in1=half_relu[:, h * width : (h + 1) * width].rearrange("p (j t) -> p j t", t=PACK),
-                op0=ALU.max,
-                op1=ALU.subtract,
+                out=hid_bf[h][:, i0 : i0 + CHUNK, :].rearrange("p j t -> p (j t)"),
+                in0=half_relu[:, j0 * PACK : (j0 + CHUNK) * PACK],
+                scalar=-0.5,
+                in1=half_relu[:, lo : lo + CHUNK * PACK],
+                op0=ALU.mult,
+                op1=ALU.add,
             )
+            if i0 + CHUNK == HALF:
+                quantize(hid_codes[h], hid_scales[h], hid_bf[h], E5M2X4)
         floor_all = sb.tile([P, HALVES, N_TILES, HALF], F32, name="floor_all", tag="u_codes1", align_bytes=64)
         floor_sb = [floor_all[:, h] for h in range(HALVES)]
         for h in range(HALVES):
@@ -184,14 +184,13 @@ def tile_list_steps_lagged_floored_kernel(tc, xf, fk, w_words, w_scales, wb, tz,
                 nc.scalar.activation(
                     floor_sb[h][:, c, :], tz_sb[:, c, :].indirect(z_list[:, h * cols : (h + 1) * cols]), ACT.Copy
                 )
-        for h in range(HALVES):
-            quantize(hid_codes[h], hid_scales[h], hid_bf[h], E5M2X4)
 
-        p_ps = [ps.tile([P, N_TILES, HALF], F32, name="p_ps%d" % h) for h in range(HALVES)]
-        for h in range(HALVES):
-            for c in range(N_TILES):
+        pieces = [(0, 0, N_TILES)] + [(1, c, 1) for c in range(N_TILES)]
+        p_ps = [ps.tile([P, n, HALF], F32, name="p_ps%d" % i) for i, (h, c0, n) in enumerate(pieces)]
+        for i, (h, c0, n) in enumerate(pieces):
+            for c in range(c0, c0 + n):
                 nc.tensor.matmul_mx(
-                    out=p_ps[h][:, c, :],
+                    out=p_ps[i][:, c - c0, :],
                     lhsT=wb_codes[c][:].bitcast(E5M2X4),
                     lhsT_scale=wb_scales[c][:],
                     rhs=hid_codes[h][:].bitcast(E5M2X4),
@@ -201,17 +200,19 @@ def tile_list_steps_lagged_floored_kernel(tc, xf, fk, w_words, w_scales, wb, tz,
                 )
 
         out_rows = out.rearrange("(c p) j -> p c j", p=P)
-        higher = [sb.tile([P, N_TILES, HALF], F32, name="higher%d" % h) for h in range(HALVES)]
-        result = [sb.tile([P, N_TILES, HALF], F32, name="result%d" % h) for h in range(HALVES)]
+        higher = [sb.tile([P, N_TILES, HALF], F32, name="higher0", tag="hid_bf1", align_bytes=64)]
+        higher.extend(sb.tile([P, 1, HALF], F32, name="higher%d" % i) for i in (1, 2))
+        result = [sb.tile([P, n, HALF], F32, name="result%d" % i) for i, (h, c0, n) in enumerate(pieces)]
         pairs = HALF // 2
-        for h in range(HALVES):
-            nc.vector.tensor_tensor(out=higher[h][:], in0=p_ps[h][:], in1=floor_sb[h], op=ALU.max)
-        for h in range(HALVES):
+        queues = (nc.sync, nc.sync, nc.scalar)
+        for i, (h, c0, n) in enumerate(pieces):
+            nc.vector.tensor_tensor(out=higher[i][:], in0=p_ps[i][:], in1=floor_sb[h][:, c0 : c0 + n, :], op=ALU.max)
+        for i, (h, c0, n) in enumerate(pieces):
             weights = rw_ps[:, :, h * pairs : (h + 1) * pairs].rearrange("p e m -> p m e")
             nc.vector.tensor_tensor(
-                out=result[h][:].rearrange("p c (m e) -> p c m e", e=2),
-                in0=higher[h][:].rearrange("p c (m e) -> p c m e", e=2),
-                in1=weights.unsqueeze(1).to_broadcast([P, N_TILES, pairs, 2]),
+                out=result[i][:].rearrange("p c (m e) -> p c m e", e=2),
+                in0=higher[i][:].rearrange("p c (m e) -> p c m e", e=2),
+                in1=weights.unsqueeze(1).to_broadcast([P, n, pairs, 2]),
                 op=ALU.mult,
             )
-            nc.sync.dma_start(out=out_rows[:, :, h * HALF : (h + 1) * HALF], in_=result[h][:])
+            queues[i].dma_start(out=out_rows[:, c0 : c0 + n, h * HALF : (h + 1) * HALF], in_=result[i][:])

@@ -39,7 +39,7 @@ def tile_list_steps_lagged_floored_kernel(tc, xf, fk, w_words, w_scales, wb, tz,
         fk_sb = sb.tile([P, PACK], F32, name="fk_sb")
         rw_sb = sb.tile([P, 2], F32, name="rw_sb")
         w_raw = sb.tile([P, R], I32, name="w_raw")
-        ws_raw = sb.tile([P, R], U8, name="ws_raw")
+        ws_raw = sb.tile([P, R], U8, name="ws_raw", tag="step1")
         wb_raw = sb.tile([P, PACK, N], F32, name="wb_raw")
         tz_sb = sb.tile([P, N_TILES, Z], F32, name="tz_sb")
         picked = [sb.tile([P, PAD + J], F32, name="picked%d" % t) for t in range(PACK)]
@@ -48,21 +48,17 @@ def tile_list_steps_lagged_floored_kernel(tc, xf, fk, w_words, w_scales, wb, tz,
 
         x_rows = xf.rearrange("(p t) c -> t p c", t=PACK)
 
-        nc.gpsimd.memset(ws_raw[:].bitcast(U32), 0)
         for t in range(PACK):
             nc.vector.memset(picked[t][:, PAD - 1 : PAD], 0.0)
-        nc.scalar.activation(
-            half_relu[:, 0 : LAG * PACK], picked[0][:, PAD - 1 : PAD].to_broadcast([P, LAG * PACK]), ACT.Relu
-        )
 
-        nc.scalar.dma_start(out=fk_sb[:], in_=fk.rearrange("(p t) o -> p (t o)", t=PACK))
-        nc.scalar.dma_start(out=rw_sb[:], in_=rw.rearrange("o (p c) -> p (o c)", c=2))
-        nc.sync.dma_start(out=x_plane[0][:], in_=x_rows[0])
         nc.sync.dma_start(x_list[:], offs)
+        nc.scalar.dma_start(out=fk_sb[:], in_=fk.rearrange("(p t) o -> p (t o)", t=PACK))
+        nc.sync.dma_start(out=x_plane[0][:], in_=x_rows[0])
         for q in range(4):
-            nc.scalar.dma_start(
-                out=ws_raw[32 * q : 32 * q + 4, :].bitcast(I32),
-                in_=w_scales[0, 4 * q : 4 * q + 4, :].bitcast(I32),
+            rows = w_scales[0, 4 * q : 4 * q + 4, :].bitcast(I32)
+            nc.sync.dma_start(
+                out=ws_raw[32 * q : 32 * (q + 1), :].bitcast(I32),
+                in_=rows.unsqueeze(0).to_broadcast([8, 4, R // 4]),
             )
         for t in range(1, PACK):
             nc.sync.dma_start(out=x_plane[t][:], in_=x_rows[t])
@@ -70,9 +66,13 @@ def tile_list_steps_lagged_floored_kernel(tc, xf, fk, w_words, w_scales, wb, tz,
         nc.sync.dma_start(out=wb_raw[:], in_=wb.rearrange("(p t) n -> p t n", t=PACK))
         nc.sync.dma_start(z_list[:], offs2)
         nc.sync.dma_start(out=tz_sb[:], in_=tz.rearrange("(c p) z -> p c z", p=P))
+        nc.sync.dma_start(out=rw_sb[:], in_=rw.rearrange("o (p c) -> p (o c)", c=2))
+        nc.scalar.activation(
+            half_relu[:, 0 : LAG * PACK], picked[0][:, PAD - 1 : PAD].to_broadcast([P, LAG * PACK]), ACT.Relu
+        )
         make_identity(nc, ident[:])
 
-        step = [sb.tile([P, J], F32, name="step%d" % t) for t in range(PACK)]
+        step = [sb.tile([P, J], F32, name="step%d" % t, tag="step%d" % t) for t in range(PACK)]
         u_bf = [sb.tile([P, HALF, PACK], BF16, name="u_bf%d" % h, tag="u_bf%d" % h, align_bytes=64) for h in range(HALVES)]
         u_codes = [sb.tile([P, HALF], U32, name="u_codes%d" % h, tag="u_codes%d" % h, align_bytes=64) for h in range(HALVES)]
         u_scales = [sb.tile([P, HALF], U8, name="u_scales%d" % h, align_bytes=64) for h in range(HALVES)]
@@ -146,14 +146,18 @@ def tile_list_steps_lagged_floored_kernel(tc, xf, fk, w_words, w_scales, wb, tz,
                     stop=True,
                 )
 
-        wb_bf = [sb.tile([P, P, PACK], BF16, name="wb_bf%d" % c, align_bytes=64) for c in range(N_TILES)]
+        wb_bf = [
+            sb.tile([P, P, PACK], BF16, name="wb_bf0", align_bytes=64),
+            sb.tile([P, P, PACK], BF16, name="wb_bf1", tag="u_bf1", align_bytes=64),
+        ]
         wb_codes = [sb.tile([P, P], U32, name="wb_codes%d" % c, align_bytes=64) for c in range(N_TILES)]
         wb_scales = [sb.tile([P, P], U8, name="wb_scales%d" % c, align_bytes=64) for c in range(N_TILES)]
-        for c in range(N_TILES):
-            nc.scalar.copy(
+        for c, copy in enumerate((nc.scalar.copy, nc.vector.tensor_copy)):
+            copy(
                 wb_bf[c][:].rearrange("p (g i) t -> p g t i", i=4),
                 wb_raw[:, :, c * P : (c + 1) * P].rearrange("p t (g i) -> p g t i", i=4),
             )
+        for c in range(N_TILES):
             quantize(wb_codes[c], wb_scales[c], wb_bf[c], E5M2X4)
 
         hid_bf = [sb.tile([P, HALF, PACK], BF16, name="hid_bf%d" % h, tag="hid_bf%d" % h, align_bytes=64) for h in range(HALVES)]

@@ -48,6 +48,7 @@ def tile_list_steps_lagged_floored_kernel(tc, xf, fk, w_words, w_scales, wb, tz,
 
         x_rows = xf.rearrange("(p t) c -> t p c", t=PACK)
 
+        nc.gpsimd.memset(ws_raw[:].bitcast(U32), 0)
         for t in range(PACK):
             nc.vector.memset(picked[t][:, PAD - 1 : PAD], 0.0)
 
@@ -55,14 +56,13 @@ def tile_list_steps_lagged_floored_kernel(tc, xf, fk, w_words, w_scales, wb, tz,
         nc.scalar.dma_start(out=fk_sb[:], in_=fk.rearrange("(p t) o -> p (t o)", t=PACK))
         nc.sync.dma_start(out=x_plane[0][:], in_=x_rows[0])
         for q in range(4):
-            rows = w_scales[0, 4 * q : 4 * q + 4, :].bitcast(I32)
             nc.sync.dma_start(
-                out=ws_raw[32 * q : 32 * (q + 1), :].bitcast(I32),
-                in_=rows.unsqueeze(0).to_broadcast([8, 4, R // 4]),
+                out=ws_raw[32 * q : 32 * q + 4, :].bitcast(I32),
+                in_=w_scales[0, 4 * q : 4 * q + 4, :].bitcast(I32),
             )
+        nc.sync.dma_start(out=w_raw[:], in_=w_words[0].rearrange("p n t -> p (n t)").bitcast(I32))
         for t in range(1, PACK):
             nc.sync.dma_start(out=x_plane[t][:], in_=x_rows[t])
-        nc.sync.dma_start(out=w_raw[:], in_=w_words[0].rearrange("p n t -> p (n t)").bitcast(I32))
         nc.sync.dma_start(out=wb_raw[:], in_=wb.rearrange("(p t) n -> p t n", t=PACK))
         nc.sync.dma_start(z_list[:], offs2)
         nc.sync.dma_start(out=tz_sb[:], in_=tz.rearrange("(c p) z -> p c z", p=P))
@@ -102,6 +102,10 @@ def tile_list_steps_lagged_floored_kernel(tc, xf, fk, w_words, w_scales, wb, tz,
             out=w_planes[:].rearrange("p (t m) -> p m t", t=PACK),
             in_=ws_raw[:].rearrange("p (m t) -> p m t", t=PACK),
         )
+        nc.vector.tensor_copy(
+            out=w_codes[:].rearrange("p (t m) -> p m t", t=PACK),
+            in_=w_raw[:].rearrange("p (m t) -> p m t", t=PACK),
+        )
         cols = HALF // 16
         last = PACK - 1
         for t in range(PACK):
@@ -119,10 +123,6 @@ def tile_list_steps_lagged_floored_kernel(tc, xf, fk, w_words, w_scales, wb, tz,
             nc.vector.quantize_mx(out=codes[:].bitcast(dtype), scales=scales[:], in_=src[:].rearrange("p c t -> p (c t)"))
 
         difference(last, 0, HALF)
-        nc.vector.tensor_copy(
-            out=w_codes[:].rearrange("p (t m) -> p m t", t=PACK),
-            in_=w_raw[:].rearrange("p (m t) -> p m t", t=PACK),
-        )
         scale_round(last, 0)
         quantize(u_codes[0], u_scales[0], u_bf[0], E4M3X4)
         difference(last, HALF, HALF)

from contextlib import ExitStack

import concourse.mybir as mybir
from concourse.masks import make_identity

K, T, J, R, N, Z = 512, 1024, 256, 512, 256, 512
FLOPS = 2 * K * R * J + 2 * R * N * J

F32 = mybir.dt.float32
BF16 = mybir.dt.bfloat16
I32 = mybir.dt.int32
U32 = mybir.dt.uint32
U16 = mybir.dt.uint16
U8 = mybir.dt.uint8
E4M3X4 = mybir.dt.float8_e4m3fn_x4
E5M2X4 = mybir.dt.float8_e5m2_x4
ALU = mybir.AluOpType
ACT = mybir.ActivationFunctionType

P = 128
PACK = 4
HALF = 128
HALVES = J // HALF
N_TILES = N // P
PAD = 8
LAG = 2
CHUNK = 64


def tile_list_steps_lagged_floored_kernel(tc, xf, fk, w_words, w_scales, wb, tz, rw, offs, offs2, out):
    nc = tc.nc
    with ExitStack() as ctx:
        sb = ctx.enter_context(tc.tile_pool(name="sb", bufs=1))
        ps = ctx.enter_context(tc.psum_pool(name="ps", bufs=1))

        x_list = sb.tile([P, J // 16], U16, name="x_list")
        z_list = sb.tile([P, J // 16], U16, name="z_list")
        x_plane = [sb.tile([P, T], F32, name="x_plane%d" % t) for t in range(PACK)]
        fk_sb = sb.tile([P, PACK], F32, name="fk_sb")
        rw_sb = sb.tile([P, 2], F32, name="rw_sb")
        w_raw = sb.tile([P, R], I32, name="w_raw")
        ws_raw = sb.tile([P, R], U8, name="ws_raw", tag="step1")
        wb_raw = sb.tile([P, PACK, N], F32, name="wb_raw")
        tz_sb = sb.tile([P, N_TILES, Z], F32, name="tz_sb")
        picked = [sb.tile([P, PAD + J], F32, name="picked%d" % t) for t in range(PACK)]
        half_relu = sb.tile([P, (LAG + J) * PACK], F32, name="half_relu")
        ident = sb.tile([P, P], F32, name="ident")

        x_rows = xf.rearrange("(p t) c -> t p c", t=PACK)

        nc.gpsimd.memset(ws_raw[:].bitcast(U32), 0)
        for t in range(PACK):
            nc.vector.memset(picked[t][:, PAD - 1 : PAD], 0.0)

        nc.sync.dma_start(x_list[:], offs)
        nc.scalar.dma_start(out=fk_sb[:], in_=fk.rearrange("(p t) o -> p (t o)", t=PACK))
        nc.sync.dma_start(out=x_plane[0][:], in_=x_rows[0])
        for q in range(4):
            nc.sync.dma_start(
                out=ws_raw[32 * q : 32 * q + 4, :].bitcast(I32),
                in_=w_scales[0, 4 * q : 4 * q + 4, :].bitcast(I32),
            )
        nc.sync.dma_start(out=w_raw[:], in_=w_words[0].rearrange("p n t -> p (n t)").bitcast(I32))
        for t in range(1, PACK):
            nc.sync.dma_start(out=x_plane[t][:], in_=x_rows[t])
        nc.sync.dma_start(out=wb_raw[:], in_=wb.rearrange("(p t) n -> p t n", t=PACK))
        nc.sync.dma_start(z_list[:], offs2)
        nc.sync.dma_start(out=tz_sb[:], in_=tz.rearrange("(c p) z -> p c z", p=P))
        nc.sync.dma_start(out=rw_sb[:], in_=rw.rearrange("o (p c) -> p (o c)", c=2))
        nc.scalar.activation(
            half_relu[:, 0 : LAG * PACK], picked[0][:, PAD - 1 : PAD].to_broadcast([P, LAG * PACK]), ACT.Relu
        )
        make_identity(nc, ident[:])

        step = [sb.tile([P, J], F32, name="step%d" % t, tag="step%d" % t) for t in range(PACK)]
        u_bf = [sb.tile([P, HALF, PACK], BF16, name="u_bf%d" % h, tag="u_bf%d" % h, align_bytes=64) for h in range(HALVES)]
        u_codes = [sb.tile([P, HALF], U32, name="u_codes%d" % h, tag="u_codes%d" % h, align_bytes=64) for h in range(HALVES)]
        u_scales = [sb.tile([P, HALF], U8, name="u_scales%d" % h, align_bytes=64) for h in range(HALVES)]
        w_codes = sb.tile([P, R], I32, name="w_codes", align_bytes=64)
        w_planes = sb.tile([P, R], U8, name="w_planes", align_bytes=64)

        def difference(t, j0, n):
            nc.vector.scalar_tensor_tensor(
                out=step[t][:, j0 : j0 + n],
                in0=picked[t][:, PAD - 1 + j0 : PAD - 1 + j0 + n],
                scalar=-0.6,
                in1=picked[t][:, PAD + j0 : PAD + j0 + n],
                op0=ALU.mult,
                op1=ALU.add,
            )

        def scale_round(t, h):
            nc.vector.tensor_scalar(
                out=u_bf[h][:, :, t],
                in0=step[t][:, h * HALF : (h + 1) * HALF],
                scalar1=fk_sb[:, t : t + 1],
                scalar2=None,
                op0=ALU.mult,
            )

        nc.vector.tensor_copy(
            out=w_planes[:].rearrange("p (t m) -> p m t", t=PACK),
            in_=ws_raw[:].rearrange("p (m t) -> p m t", t=PACK),
        )
        nc.vector.tensor_copy(
            out=w_codes[:].rearrange("p (t m) -> p m t", t=PACK),
            in_=w_raw[:].rearrange("p (m t) -> p m t", t=PACK),
        )
        cols = HALF // 16
        last = PACK - 1
        for t in range(PACK):
            for h in range(HALVES):
                nc.scalar.activation(
                    picked[t][:, PAD + h * HALF : PAD + (h + 1) * HALF],
                    x_plane[t][:].indirect(x_list[:, h * cols : (h + 1) * cols]),
                    ACT.Copy,
                )
                if t < last:
                    difference(t, h * HALF, HALF)
                    scale_round(t, h)

        def quantize(codes, scales, src, dtype):
            nc.vector.quantize_mx(out=codes[:].bitcast(dtype), scales=scales[:], in_=src[:].rearrange("p c t -> p (c t)"))

        difference(last, 0, HALF)
        scale_round(last, 0)
        quantize(u_codes[0], u_scales[0], u_bf[0], E4M3X4)
        difference(last, HALF, HALF)
        scale_round(last, 1)
        quantize(u_codes[1], u_scales[1], u_bf[1], E4M3X4)

        rw_ps = ps.tile([P, 2, P], F32, name="rw_ps")
        for c in range(2):
            nc.tensor.transpose(rw_ps[:, c, :], rw_sb[:, c : c + 1].to_broadcast([P, P]), ident[:])

        a_ps = [ps.tile([P, PACK, HALF], F32, name="a_ps%d" % h) for h in range(HALVES)]
        for h in range(HALVES):
            for t in range(PACK):
                nc.tensor.matmul_mx(
                    out=a_ps[h][:, t, :],
                    lhsT=w_codes[:, t * P : (t + 1) * P].bitcast(E5M2X4),
                    lhsT_scale=w_planes[:, t * P : (t + 1) * P],
                    rhs=u_codes[h][:].bitcast(E4M3X4),
                    rhs_scale=u_scales[h][:],
                    start=True,
                    stop=True,
                )

        wb_bf = [
            sb.tile([P, P, PACK], BF16, name="wb_bf0", align_bytes=64),
            sb.tile([P, P, PACK], BF16, name="wb_bf1", tag="u_bf1", align_bytes=64),
        ]
        wb_codes = [sb.tile([P, P], U32, name="wb_codes%d" % c, align_bytes=64) for c in range(N_TILES)]
        wb_scales = [sb.tile([P, P], U8, name="wb_scales%d" % c, align_bytes=64) for c in range(N_TILES)]
        for c, copy in enumerate((nc.scalar.copy, nc.vector.tensor_copy)):
            copy(
                wb_bf[c][:].rearrange("p (g i) t -> p g t i", i=4),
                wb_raw[:, :, c * P : (c + 1) * P].rearrange("p t (g i) -> p g t i", i=4),
            )
        for c in range(N_TILES):
            quantize(wb_codes[c], wb_scales[c], wb_bf[c], E5M2X4)

        hid_bf = [sb.tile([P, HALF, PACK], BF16, name="hid_bf%d" % h, tag="hid_bf%d" % h, align_bytes=64) for h in range(HALVES)]
        hid_codes = [sb.tile([P, HALF], U32, name="hid_codes%d" % h, align_bytes=64) for h in range(HALVES)]
        hid_scales = [sb.tile([P, HALF], U8, name="hid_scales%d" % h, align_bytes=64) for h in range(HALVES)]
        for j0 in range(0, J, CHUNK):
            h, i0 = divmod(j0, HALF)
            lo = (LAG + j0) * PACK
            nc.scalar.activation(
                half_relu[:, lo : lo + CHUNK * PACK].rearrange("p (j t) -> p j t", t=PACK),
                a_ps[h][:, :, i0 : i0 + CHUNK].rearrange("p t j -> p j t"),
                ACT.Relu,
            )
            nc.vector.scalar_tensor_tensor(
                out=hid_bf[h][:, i0 : i0 + CHUNK, :].rearrange("p j t -> p (j t)"),
                in0=half_relu[:, j0 * PACK : (j0 + CHUNK) * PACK],
                scalar=-0.5,
                in1=half_relu[:, lo : lo + CHUNK * PACK],
                op0=ALU.mult,
                op1=ALU.add,
            )
            if i0 + CHUNK == HALF:
                quantize(hid_codes[h], hid_scales[h], hid_bf[h], E5M2X4)
        floor_all = sb.tile([P, HALVES, N_TILES, HALF], F32, name="floor_all", tag="u_codes1", align_bytes=64)
        floor_sb = [floor_all[:, h] for h in range(HALVES)]
        for h in range(HALVES):
            for c in range(N_TILES):
                nc.scalar.activation(
                    floor_sb[h][:, c, :], tz_sb[:, c, :].indirect(z_list[:, h * cols : (h + 1) * cols]), ACT.Copy
                )

        pieces = [(0, 0, N_TILES)] + [(1, c, 1) for c in range(N_TILES)]
        p_ps = [ps.tile([P, n, HALF], F32, name="p_ps%d" % i) for i, (h, c0, n) in enumerate(pieces)]
        for i, (h, c0, n) in enumerate(pieces):
            for c in range(c0, c0 + n):
                nc.tensor.matmul_mx(
                    out=p_ps[i][:, c - c0, :],
                    lhsT=wb_codes[c][:].bitcast(E5M2X4),
                    lhsT_scale=wb_scales[c][:],
                    rhs=hid_codes[h][:].bitcast(E5M2X4),
                    rhs_scale=hid_scales[h][:],
                    start=True,
                    stop=True,
                )

        out_rows = out.rearrange("(c p) j -> p c j", p=P)
        higher = [sb.tile([P, N_TILES, HALF], F32, name="higher0", tag="hid_bf1", align_bytes=64)]
        higher.extend(sb.tile([P, 1, HALF], F32, name="higher%d" % i) for i in (1, 2))
        result = [sb.tile([P, n, HALF], F32, name="result%d" % i) for i, (h, c0, n) in enumerate(pieces)]
        pairs = HALF // 2
        queues = (nc.sync, nc.sync, nc.scalar)
        for i, (h, c0, n) in enumerate(pieces):
            nc.vector.tensor_tensor(out=higher[i][:], in0=p_ps[i][:], in1=floor_sb[h][:, c0 : c0 + n, :], op=ALU.max)
        for i, (h, c0, n) in enumerate(pieces):
            weights = rw_ps[:, :, h * pairs : (h + 1) * pairs].rearrange("p e m -> p m e")
            nc.vector.tensor_tensor(
                out=result[i][:].rearrange("p c (m e) -> p c m e", e=2),
                in0=higher[i][:].rearrange("p c (m e) -> p c m e", e=2),
                in1=weights.unsqueeze(1).to_broadcast([P, n, pairs, 2]),
                op=ALU.mult,
            )
            queues[i].dma_start(out=out_rows[:, c0 : c0 + n, h * HALF : (h + 1) * HALF], in_=result[i][:])
